import numpy as np
import ml_dtypes


def mxq(x, axis, fmt="e4m3"):
    dtype, down = {"e4m3": (ml_dtypes.float8_e4m3fn, 7), "e5m2": (ml_dtypes.float8_e5m2, 14)}[fmt]
    v = np.moveaxis(np.asarray(x, np.float32).astype(ml_dtypes.bfloat16).astype(np.float64), axis, -1)
    blocks = v.reshape(v.shape[:-1] + (-1, 32))
    amax = np.abs(blocks).max(-1, keepdims=True)
    byte = np.maximum(np.where(amax > 0, np.frexp(amax)[1] - 1 + 127, 0) - down, 1)
    scale = np.exp2(byte - 127.0)
    codes = (blocks / scale).astype(np.float32).astype(dtype).astype(np.float64)
    return np.moveaxis((codes * scale).reshape(v.shape), -1, axis)


WIDE = False


def mx_kscale(k):
    if not WIDE:
        return np.ones(k)
    levels = np.array([10, -10, 5, -5, 0])
    if k % 512:
        return np.exp2(np.random.permutation(np.resize(levels, k // 32))).repeat(32)
    a = np.empty((k // 512, 16))
    for p in range(k // 512):
        a[p, :8] = np.random.permutation(np.resize(levels, 8))
        for g in range(8):
            far = levels[np.abs(levels - a[p, g]) >= 10]
            a[p, g + 8] = far[np.random.randint(len(far))]
    return np.exp2(a.ravel()).repeat(32)


def f64(x):
    return np.asarray(x).astype(np.float64)


def striped(idx):
    return np.tile(idx.reshape(-1, 16).T, (8, 1)).astype(np.uint16)


def unstriped(offs):
    return offs[:16].T.reshape(-1).astype(np.int64)


def striped8(idx):
    return np.concatenate([x.reshape(-1, 16).T for x in idx]).astype(np.uint16)


def runs(offs, k):
    lists = np.stack([offs[16 * r : 16 * r + 16].T.reshape(-1) for r in range(8)]).astype(np.int64)
    return lists[np.arange(k) % 512 // 64]


def pack_weight(w):
    k, n = w.shape
    w = f64(np.asarray(w, np.float32).astype(ml_dtypes.bfloat16)).reshape(k // 32, 32, n)
    amax = np.abs(w).max(1)
    byte = np.clip(np.where(amax > 0, np.frexp(amax)[1] - 1 + 127 - 7, 1), 1, 254)
    scaled = (w * np.exp2(127.0 - byte)[:, None, :]).reshape(k, n).astype(np.float32)
    words = np.ascontiguousarray(scaled.reshape(k // 512, 128, 4, n).transpose(0, 1, 3, 2)).astype(ml_dtypes.float8_e4m3fn).view(np.uint8)
    return words, np.ascontiguousarray(byte.astype(np.uint8).reshape(k // 512, 16, n))


def unpack_weight(words, scales):
    g, p, n, _ = words.shape
    vals = np.ascontiguousarray(words).view(ml_dtypes.float8_e4m3fn).astype(np.float64) * np.repeat(np.exp2(scales.astype(np.float64) - 127.0), 8, axis=1)[..., None]
    return vals.transpose(0, 1, 3, 2).reshape(g * 512, n)


def sigmoid(v):
    return 1.0 / (1.0 + np.exp(-np.maximum(v, -700.0)))

def planes(y):
    n, m = y.shape
    v = y.astype(np.float32).astype(ml_dtypes.bfloat16).astype(np.float64).reshape(n // 32, 32, m)
    top = np.abs(v).max(1)
    byte = np.clip(np.where(top > 0, np.frexp(top)[1] - 1 + 127 - 7, 1), 1, 254)
    codes = (v * np.exp2(127.0 - byte)[:, None, :]).reshape(n, m).astype(np.float32).astype(ml_dtypes.float8_e4m3fn).view(np.uint8)
    words = codes.reshape(n // 512, 128, 4, m).transpose(0, 1, 3, 2)
    return np.ascontiguousarray(words), np.ascontiguousarray(byte.astype(np.uint8).reshape(n // 512, 16, m))


K, T, S, N, H = 512, 2048, 512, 512, 512


def setup_inputs():
    n = np.random.standard_normal
    s = mx_kscale(K)[:, None]
    u = mx_kscale(H)
    packed_xT = pack_weight(n((K, T)) * s)
    packed_w1 = pack_weight(n((K, H)) / np.sqrt(K) / s)
    packed_w2 = pack_weight(n((H, N)) / np.sqrt(H) / u[:, None])
    return {
        "x_words": packed_xT[0],
        "x_scales": packed_xT[1],
        "w1_words": packed_w1[0],
        "w1_scales": packed_w1[1],
        "gn": (np.random.uniform(0.5, 1.5, (H, 1)) * u[:, None]).astype(np.float32),
        "w2_words": packed_w2[0],
        "w2_scales": packed_w2[1],
        "offs": striped(np.random.permutation(T)[:S]),
        "pos": striped8(np.stack([np.random.permutation(S) for _ in range(8)])),
        "neg": striped8(np.stack([np.random.permutation(S) for _ in range(8)])),
    }


def reference(x_words, x_scales, w1_words, w1_scales, gn, w2_words, w2_scales, offs, pos, neg):
    xq = unpack_weight(x_words, x_scales)[:, unstriped(offs)]
    p = np.clip(sigmoid(unpack_weight(w1_words, w1_scales).T @ xq), 0.05, 0.95)
    w = -1.0 * (p[np.arange(H)[:, None], runs(pos, H)]) + 1
    z = f64(gn) * (((w) ** 2) * (-1.0 * (np.log(p[np.arange(H)[:, None], runs(pos, H)]))) - (((p[np.arange(H)[:, None], runs(neg, H)]) ** 2) * (-1.0 * (np.log(-1.0 * (p[np.arange(H)[:, None], runs(neg, H)]) + 1)))))
    out_0 = unpack_weight(w2_words, w2_scales).T @ mxq(z, 0, "e4m3")
    return (out_0,) + planes(out_0)

@@ -1,0 +1,190 @@
+from contextlib import ExitStack
+
+import concourse.mybir as mybir
+
+K, T, S, N, H = 512, 2048, 512, 512, 512
+FLOPS = 2 * K * H * S + 2 * H * N * S
+
+F32 = mybir.dt.float32
+BF16 = mybir.dt.bfloat16
+I32 = mybir.dt.int32
+U32 = mybir.dt.uint32
+U16 = mybir.dt.uint16
+U8 = mybir.dt.uint8
+FP8X4 = mybir.dt.float8_e4m3fn_x4
+ALU = mybir.AluOpType
+ACT = mybir.ActivationFunctionType
+
+P = 128
+PACK = 4
+LANES = 16
+HALF = S // 2
+PIECE = 128
+P_LOW, P_HIGH = 0.05, 0.95
+
+
+def words_view(dram):
+    return dram[0].rearrange("p c r -> p (c r)").bitcast(I32)
+
+
+def load_scale_rows(queues, plane, dram):
+    for q, queue in enumerate(queues):
+        queue.dma_start(out=plane[32 * q : 32 * q + 4, :].bitcast(I32), in_=dram[0, 4 * q : 4 * q + 4, :].bitcast(I32))
+
+
+def deal_columns(nc, dst, src, run):
+    nc.vector.tensor_copy(
+        out=dst[:].rearrange("p (t c i) -> p c t i", t=PACK, i=run),
+        in_=src[:].rearrange("p (c i t) -> p c t i", t=PACK, i=run),
+    )
+
+
+def interleave(engine_copy, dst, src):
+    engine_copy(
+        out=dst[:].rearrange("p (c i) t -> p c t i", i=4),
+        in_=src[:].rearrange("p t (c i) -> p c t i", i=4),
+    )
+
+
+def list_slice(lst, start, count):
+    return lst[:, start // LANES : (start + count) // LANES]
+
+
+def tile_picked_focalpair_none_po_kernel(
+    tc, x_words, x_scales, w1_words, w1_scales, gn, w2_words, w2_scales, offs, pos, neg, out_0, out_1, out_2
+):
+    nc = tc.nc
+    with ExitStack() as ctx:
+        keep = ctx.enter_context(tc.tile_pool(name="keep", bufs=1))
+        rows = ctx.enter_context(tc.tile_pool(name="rows", bufs=PACK))
+        psum = ctx.enter_context(tc.psum_pool(name="psum", bufs=PACK))
+
+        offs_sb = keep.tile([P, S // LANES], U16)
+        pos_sb = keep.tile([P, S // LANES], U16)
+        neg_sb = keep.tile([P, S // LANES], U16)
+        xw = keep.tile([P, T], I32, align_bytes=64)
+        xs = keep.tile([P, T], U8, align_bytes=64)
+        w_raw = keep.tile([P, H], I32, align_bytes=64)
+        ws_raw = keep.tile([P, H], U8, align_bytes=64)
+        gain = keep.tile([P, PACK], F32)
+        one = keep.tile([P, 1], F32)
+
+        nc.vector.memset(xs[:].bitcast(I32), 0)
+        nc.vector.memset(ws_raw[:].bitcast(I32), 0)
+        nc.vector.memset(one[:], 1.0)
+
+        nc.sync.dma_start(offs_sb[:], offs)
+        nc.sync.dma_start(pos_sb[:], pos)
+        nc.sync.dma_start(neg_sb[:], neg)
+        nc.sync.dma_start(out=gain[:], in_=gn.rearrange("(p t) o -> p (t o)", t=PACK))
+        nc.sync.dma_start(out=w_raw[:], in_=words_view(w1_words))
+        nc.sync.dma_start(out=xw[:], in_=words_view(x_words))
+        load_scale_rows([nc.scalar] * 4, xs, x_scales)
+        load_scale_rows([nc.gpsimd, nc.gpsimd, nc.sync, nc.sync], ws_raw, w1_scales)
+
+        w1 = keep.tile([P, H], I32, align_bytes=64)
+        w1s = keep.tile([P, H], U8, align_bytes=64)
+        w2 = keep.tile([P, N], I32, align_bytes=64)
+        w2s = keep.tile([P, N], U8, align_bytes=64)
+        xg = keep.tile([P, S], U32, align_bytes=64)
+        xgs = keep.tile([P, S], U8, align_bytes=64)
+
+        nc.vector.tensor_copy(xgs[:], xs[:].indirect(offs_sb[:]))
+        deal_columns(nc, w1, w_raw, 4)
+        deal_columns(nc, w1s, ws_raw, 16)
+        nc.sync.dma_start(out=w_raw[:], in_=words_view(w2_words))
+        load_scale_rows([nc.sync] * 4, ws_raw, w2_scales)
+
+        h = [psum.tile([P, S], F32, name="h") for t in range(PACK)]
+        for lo in range(0, S, HALF):
+            cols = slice(lo, lo + HALF)
+            nc.vector.tensor_copy(xg[:, cols], xw[:].bitcast(U32).indirect(list_slice(offs_sb, lo, HALF)))
+            for t in range(PACK):
+                feat = slice(t * P, (t + 1) * P)
+                nc.tensor.matmul_mx(
+                    out=h[t][:, cols],
+                    lhsT=w1[:, feat].bitcast(FP8X4),
+                    lhsT_scale=w1s[:, feat],
+                    rhs=xg[:, cols].bitcast(FP8X4),
+                    rhs_scale=xgs[:, cols],
+                    start=True,
+                    stop=True,
+                )
+
+        prob = []
+        p_pos = keep.tile([P, PACK, S], F32)
+        for t in range(PACK):
+            sig = rows.tile([P, S], F32)
+            nc.scalar.activation(sig[:], h[t][:], ACT.Sigmoid)
+            p_t = rows.tile([P, S], F32)
+            nc.vector.tensor_scalar(p_t[:], sig[:], P_LOW, P_HIGH, ALU.max, ALU.min)
+            for lo in range(0, S, HALF):
+                nc.vector.tensor_copy(p_pos[:, t, lo : lo + HALF], p_t[:].indirect(list_slice(pos_sb, lo, HALF)))
+            prob.append(p_t)
+
+        deal_columns(nc, w2, w_raw, 4)
+        deal_columns(nc, w2s, ws_raw, 16)
+
+        neg_term = []
+        for t in range(PACK):
+            log_q = rows.tile([P, S], F32)
+            nc.scalar.activation(log_q[:], prob[t][:], ACT.Ln, bias=one[:], scale=-1.0)
+            p_sq = rows.tile([P, S], F32)
+            nc.scalar.activation(p_sq[:], prob[t][:], ACT.Square)
+            b_t = rows.tile([P, S], F32)
+            nc.vector.scalar_tensor_tensor(b_t[:], p_sq[:], gain[:, t : t + 1], log_q[:], ALU.mult, ALU.mult)
+            neg_term.append(b_t)
+
+        y_codes = keep.tile([P, S], I32, align_bytes=64)
+        y_scales = keep.tile([P, S], U8, align_bytes=64)
+        out_rows = out_0.rearrange("(p t) j -> p t j", t=PACK)
+        for lo in range(0, S, PIECE):
+            cols = slice(lo, lo + PIECE)
+            log_p = rows.tile([P, PACK, PIECE], F32)
+            nc.scalar.activation(log_p[:], p_pos[:, :, cols], ACT.Ln)
+            w_sq = rows.tile([P, PACK, PIECE], F32)
+            nc.scalar.activation(w_sq[:], p_pos[:, :, cols], ACT.Square, bias=one[:], scale=-1.0)
+            pos_term = rows.tile([P, PACK, PIECE], F32)
+            for t in range(PACK):
+                nc.vector.scalar_tensor_tensor(
+                    pos_term[:, t, :], w_sq[:, t, :], gain[:, t : t + 1], log_p[:, t, :], ALU.mult, ALU.mult
+                )
+            z = rows.tile([P, PACK, PIECE], F32)
+            z_bf = rows.tile([P, PIECE, PACK], BF16, align_bytes=64)
+            for t in range(PACK):
+                nc.vector.tensor_tensor(
+                    z[:, t, :], neg_term[t][:].indirect(list_slice(neg_sb, lo, PIECE)), pos_term[:, t, :], ALU.subtract
+                )
+            interleave(nc.vector.tensor_copy, z_bf, z)
+            z_codes = rows.tile([P, PIECE], I32, align_bytes=64)
+            z_scales = rows.tile([P, PIECE], U8, align_bytes=64)
+            nc.vector.quantize_mx(
+                out=z_codes[:].bitcast(FP8X4), scales=z_scales[:], in_=z_bf[:].rearrange("p j t -> p (j t)")
+            )
+            acc = psum.tile([P, PACK, PIECE], F32)
+            for t in range(PACK):
+                feat = slice(t * P, (t + 1) * P)
+                nc.tensor.matmul_mx(
+                    out=acc[:, t, :],
+                    lhsT=w2[:, feat].bitcast(FP8X4),
+                    lhsT_scale=w2s[:, feat],
+                    rhs=z_codes[:].bitcast(FP8X4),
+                    rhs_scale=z_scales[:],
+                    start=True,
+                    stop=True,
+                )
+            y = rows.tile([P, PACK, PIECE], F32)
+            nc.scalar.copy(out=y[:], in_=acc[:])
+            nc.sync.dma_start(out=out_rows[:, :, cols], in_=y[:])
+            y_bf = rows.tile([P, PIECE, PACK], BF16, align_bytes=64)
+            if lo + PIECE < S:
+                nc.scalar.copy(out=y_bf[:], in_=acc[:].rearrange("p t j -> p j t"))
+            else:
+                interleave(nc.vector.tensor_copy, y_bf, y)
+            nc.vector.quantize_mx(
+                out=y_codes[:, cols].bitcast(FP8X4), scales=y_scales[:, cols], in_=y_bf[:].rearrange("p j t -> p (j t)")
+            )
+            nc.sync.dma_start(out=words_view(out_1)[:, cols], in_=y_codes[:, cols])
+        for q in range(4):
+            queue = nc.sync if q % 2 == 0 else nc.scalar
+            queue.dma_start(out=out_2[0, 4 * q : 4 * q + 4, :].bitcast(I32), in_=y_scales[32 * q : 32 * q + 4, :].bitcast(I32))

@@ -1,3 +1,4 @@
+import math
 from contextlib import ExitStack
 
 import concourse.mybir as mybir
@@ -21,28 +22,32 @@ LANES = 16
 HALF = S // 2
 PIECE = 128
 P_LOW, P_HIGH = 0.05, 0.95
+LOGIT_HIGH = math.log(P_HIGH / P_LOW)
 
 
 def words_view(dram):
     return dram[0].rearrange("p c r -> p (c r)").bitcast(I32)
 
 
-def load_scale_rows(queues, plane, dram):
-    for q, queue in enumerate(queues):
-        queue.dma_start(out=plane[32 * q : 32 * q + 4, :].bitcast(I32), in_=dram[0, 4 * q : 4 * q + 4, :].bitcast(I32))
+def load_scale_quadrant(queue, plane, dram, q):
+    rows = dram[0, 4 * q : 4 * q + 4, :].bitcast(I32)
+    queue.dma_start(
+        out=plane[32 * q : 32 * (q + 1), :].bitcast(I32),
+        in_=rows.unsqueeze(0).to_broadcast([8, 4, rows.shape[1]]),
+    )
 
 
-def deal_columns(nc, dst, src, run):
+def deal_columns(nc, dst, src, run, tiles=slice(0, PACK)):
     nc.vector.tensor_copy(
-        out=dst[:].rearrange("p (t c i) -> p c t i", t=PACK, i=run),
-        in_=src[:].rearrange("p (c i t) -> p c t i", t=PACK, i=run),
+        out=dst[:].rearrange("p (t c i) -> p c t i", t=PACK, i=run)[:, :, tiles, :],
+        in_=src[:].rearrange("p (c i t) -> p c t i", t=PACK, i=run)[:, :, tiles, :],
     )
 
 
 def interleave(engine_copy, dst, src):
     engine_copy(
-        out=dst[:].rearrange("p (c i) t -> p c t i", i=4),
-        in_=src[:].rearrange("p t (c i) -> p c t i", i=4),
+        out=dst.rearrange("p (c i) t -> p c t i", i=4),
+        in_=src.rearrange("p t (c i) -> p c t i", i=4),
     )
 
 
@@ -64,23 +69,28 @@ def tile_picked_focalpair_none_po_kernel(
         neg_sb = keep.tile([P, S // LANES], U16)
         xw = keep.tile([P, T], I32, align_bytes=64)
         xs = keep.tile([P, T], U8, align_bytes=64)
-        w_raw = keep.tile([P, H], I32, align_bytes=64)
-        ws_raw = keep.tile([P, H], U8, align_bytes=64)
+        w1_raw = keep.tile([P, H], I32, align_bytes=64)
+        w1s_raw = keep.tile([P, H], U8, align_bytes=64)
+        w2_raw = keep.tile([P, N], I32, align_bytes=64)
+        w2s_raw = keep.tile([P, N], U8, align_bytes=64)
         gain = keep.tile([P, PACK], F32)
         one = keep.tile([P, 1], F32)
-
-        nc.vector.memset(xs[:].bitcast(I32), 0)
-        nc.vector.memset(ws_raw[:].bitcast(I32), 0)
         nc.vector.memset(one[:], 1.0)
 
         nc.sync.dma_start(offs_sb[:], offs)
-        nc.sync.dma_start(pos_sb[:], pos)
-        nc.sync.dma_start(neg_sb[:], neg)
-        nc.sync.dma_start(out=gain[:], in_=gn.rearrange("(p t) o -> p (t o)", t=PACK))
-        nc.sync.dma_start(out=w_raw[:], in_=words_view(w1_words))
+        load_scale_quadrant(nc.sync, w1s_raw, w1_scales, 0)
+        for q in range(4):
+            load_scale_quadrant(nc.sync, xs, x_scales, q)
         nc.sync.dma_start(out=xw[:], in_=words_view(x_words))
-        load_scale_rows([nc.scalar] * 4, xs, x_scales)
-        load_scale_rows([nc.gpsimd, nc.gpsimd, nc.sync, nc.sync], ws_raw, w1_scales)
+        nc.sync.dma_start(out=w1_raw[:], in_=words_view(w1_words))
+        for q in range(1, 4):
+            load_scale_quadrant(nc.sync, w1s_raw, w1_scales, q)
+        nc.sync.dma_start(pos_sb[:], pos)
+        nc.sync.dma_start(out=w2_raw[:], in_=words_view(w2_words))
+        for q in range(4):
+            load_scale_quadrant(nc.sync, w2s_raw, w2_scales, q)
+        nc.sync.dma_start(out=gain[:], in_=gn.rearrange("(p t) o -> p (t o)", t=PACK))
+        nc.sync.dma_start(neg_sb[:], neg)
 
         w1 = keep.tile([P, H], I32, align_bytes=64)
         w1s = keep.tile([P, H], U8, align_bytes=64)
@@ -90,72 +100,68 @@ def tile_picked_focalpair_none_po_kernel(
         xgs = keep.tile([P, S], U8, align_bytes=64)
 
         nc.vector.tensor_copy(xgs[:], xs[:].indirect(offs_sb[:]))
-        deal_columns(nc, w1, w_raw, 4)
-        deal_columns(nc, w1s, ws_raw, 16)
-        nc.sync.dma_start(out=w_raw[:], in_=words_view(w2_words))
-        load_scale_rows([nc.sync] * 4, ws_raw, w2_scales)
+        deal_columns(nc, w1s, w1s_raw, 16)
+        nc.vector.tensor_copy(xg[:], xw[:].bitcast(U32).indirect(offs_sb[:]))
+        deal_columns(nc, w1, w1_raw, 4, slice(0, 2))
+        deal_columns(nc, w1, w1_raw, 4, slice(2, 4))
 
         h = [psum.tile([P, S], F32, name="h") for t in range(PACK)]
-        for lo in range(0, S, HALF):
-            cols = slice(lo, lo + HALF)
-            nc.vector.tensor_copy(xg[:, cols], xw[:].bitcast(U32).indirect(list_slice(offs_sb, lo, HALF)))
-            for t in range(PACK):
-                feat = slice(t * P, (t + 1) * P)
-                nc.tensor.matmul_mx(
-                    out=h[t][:, cols],
-                    lhsT=w1[:, feat].bitcast(FP8X4),
-                    lhsT_scale=w1s[:, feat],
-                    rhs=xg[:, cols].bitcast(FP8X4),
-                    rhs_scale=xgs[:, cols],
-                    start=True,
-                    stop=True,
-                )
-
-        prob = []
-        p_pos = keep.tile([P, PACK, S], F32)
         for t in range(PACK):
+            feat = slice(t * P, (t + 1) * P)
+            nc.tensor.matmul_mx(
+                out=h[t][:],
+                lhsT=w1[:, feat].bitcast(FP8X4),
+                lhsT_scale=w1s[:, feat],
+                rhs=xg[:].bitcast(FP8X4),
+                rhs_scale=xgs[:],
+                start=True,
+                stop=True,
+            )
+
+        prob = [rows.tile([P, S], F32, name="prob") for t in range(PACK)]
+        p_pos = keep.tile([P, PACK, S], F32)
+        logit = keep.tile([P, S], F32)
+        nc.vector.tensor_scalar(logit[:], h[0][:], -LOGIT_HIGH, LOGIT_HIGH, ALU.max, ALU.min)
+        for t in range(1, PACK):
             sig = rows.tile([P, S], F32)
             nc.scalar.activation(sig[:], h[t][:], ACT.Sigmoid)
-            p_t = rows.tile([P, S], F32)
-            nc.vector.tensor_scalar(p_t[:], sig[:], P_LOW, P_HIGH, ALU.max, ALU.min)
+            nc.vector.tensor_scalar(prob[t][:], sig[:], P_LOW, P_HIGH, ALU.max, ALU.min)
             for lo in range(0, S, HALF):
-                nc.vector.tensor_copy(p_pos[:, t, lo : lo + HALF], p_t[:].indirect(list_slice(pos_sb, lo, HALF)))
-            prob.append(p_t)
+                nc.vector.tensor_copy(p_pos[:, t, lo : lo + HALF], prob[t][:].indirect(list_slice(pos_sb, lo, HALF)))
+        nc.scalar.activation(prob[0][:], logit[:], ACT.Sigmoid)
+        for lo in range(0, S, HALF):
+            nc.scalar.activation(p_pos[:, 0, lo : lo + HALF], logit[:].indirect(list_slice(pos_sb, lo, HALF)), ACT.Sigmoid)
 
-        deal_columns(nc, w2, w_raw, 4)
-        deal_columns(nc, w2s, ws_raw, 16)
+        deal_columns(nc, w2, w2_raw, 4)
+        deal_columns(nc, w2s, w2s_raw, 16)
 
-        neg_term = []
-        for t in range(PACK):
-            log_q = rows.tile([P, S], F32)
-            nc.scalar.activation(log_q[:], prob[t][:], ACT.Ln, bias=one[:], scale=-1.0)
-            p_sq = rows.tile([P, S], F32)
-            nc.scalar.activation(p_sq[:], prob[t][:], ACT.Square)
-            b_t = rows.tile([P, S], F32)
-            nc.vector.scalar_tensor_tensor(b_t[:], p_sq[:], gain[:, t : t + 1], log_q[:], ALU.mult, ALU.mult)
-            neg_term.append(b_t)
+        def positive_factors(log_p, w_sq, src):
+            nc.scalar.activation(log_p, src, ACT.Ln)
+            nc.scalar.activation(w_sq, src, ACT.Square, bias=one[:], scale=-1.0)
+
+        def gained_product(out, square, log, t):
+            nc.vector.scalar_tensor_tensor(out, square, gain[:, t : t + 1], log, ALU.mult, ALU.mult)
+
+        log_p = keep.tile([P, PACK, S], F32)
+        w_sq = keep.tile([P, PACK, S], F32)
+        pos_term = keep.tile([P, PACK, S], F32)
+        z = keep.tile([P, PACK, S], F32)
+        neg_term = [rows.tile([P, S], F32, name="neg_term") for t in range(PACK)]
+
+        def difference(t, lo, count):
+            cols = slice(lo, lo + count)
+            nc.vector.tensor_tensor(
+                z[:, t, cols], neg_term[t][:].indirect(list_slice(neg_sb, lo, count)), pos_term[:, t, cols], ALU.subtract
+            )
 
         y_codes = keep.tile([P, S], I32, align_bytes=64)
         y_scales = keep.tile([P, S], U8, align_bytes=64)
         out_rows = out_0.rearrange("(p t) j -> p t j", t=PACK)
-        for lo in range(0, S, PIECE):
+
+        def second_layer(lo, cast):
             cols = slice(lo, lo + PIECE)
-            log_p = rows.tile([P, PACK, PIECE], F32)
-            nc.scalar.activation(log_p[:], p_pos[:, :, cols], ACT.Ln)
-            w_sq = rows.tile([P, PACK, PIECE], F32)
-            nc.scalar.activation(w_sq[:], p_pos[:, :, cols], ACT.Square, bias=one[:], scale=-1.0)
-            pos_term = rows.tile([P, PACK, PIECE], F32)
-            for t in range(PACK):
-                nc.vector.scalar_tensor_tensor(
-                    pos_term[:, t, :], w_sq[:, t, :], gain[:, t : t + 1], log_p[:, t, :], ALU.mult, ALU.mult
-                )
-            z = rows.tile([P, PACK, PIECE], F32)
             z_bf = rows.tile([P, PIECE, PACK], BF16, align_bytes=64)
-            for t in range(PACK):
-                nc.vector.tensor_tensor(
-                    z[:, t, :], neg_term[t][:].indirect(list_slice(neg_sb, lo, PIECE)), pos_term[:, t, :], ALU.subtract
-                )
-            interleave(nc.vector.tensor_copy, z_bf, z)
+            interleave(cast, z_bf[:], z[:, :, cols])
             z_codes = rows.tile([P, PIECE], I32, align_bytes=64)
             z_scales = rows.tile([P, PIECE], U8, align_bytes=64)
             nc.vector.quantize_mx(
@@ -173,18 +179,45 @@ def tile_picked_focalpair_none_po_kernel(
                     start=True,
                     stop=True,
                 )
+            return acc
+
+        def hand_out(lo, acc):
+            cols = slice(lo, lo + PIECE)
             y = rows.tile([P, PACK, PIECE], F32)
             nc.scalar.copy(out=y[:], in_=acc[:])
             nc.sync.dma_start(out=out_rows[:, :, cols], in_=y[:])
             y_bf = rows.tile([P, PIECE, PACK], BF16, align_bytes=64)
-            if lo + PIECE < S:
+            if lo < HALF:
                 nc.scalar.copy(out=y_bf[:], in_=acc[:].rearrange("p t j -> p j t"))
             else:
-                interleave(nc.vector.tensor_copy, y_bf, y)
+                interleave(nc.vector.tensor_copy, y_bf[:], y[:])
             nc.vector.quantize_mx(
                 out=y_codes[:, cols].bitcast(FP8X4), scales=y_scales[:, cols], in_=y_bf[:].rearrange("p j t -> p (j t)")
             )
             nc.sync.dma_start(out=words_view(out_1)[:, cols], in_=y_codes[:, cols])
+
+        first, second = slice(0, HALF), slice(HALF, S)
+        for t in (1, 2, 3, 0):
+            log_q = rows.tile([P, S], F32)
+            nc.scalar.activation(log_q[:], prob[t][:], ACT.Ln, bias=one[:], scale=-1.0)
+            p_sq = rows.tile([P, S], F32)
+            nc.scalar.activation(p_sq[:], prob[t][:], ACT.Square)
+            gained_product(neg_term[t][:], p_sq[:], log_q[:], t)
+            positive_factors(log_p[:, t, first], w_sq[:, t, first], p_pos[:, t, first])
+            gained_product(pos_term[:, t, first], w_sq[:, t, first], log_p[:, t, first], t)
+            difference(t, 0, HALF)
+        accs = [second_layer(lo, nc.vector.tensor_copy) for lo in (0, PIECE)]
+        positive_factors(log_p[:, :, second], w_sq[:, :, second], p_pos[:, :, second])
+        for t in range(PACK):
+            gained_product(pos_term[:, t, second], w_sq[:, t, second], log_p[:, t, second], t)
+        hand_out(0, accs[0])
+        hand_out(PIECE, accs[1])
+        for lo, cast in ((HALF, nc.scalar.copy), (HALF + PIECE, nc.vector.tensor_copy)):
+            for t in range(PACK):
+                difference(t, lo, PIECE)
+            accs.append(second_layer(lo, cast))
+        hand_out(HALF, accs[2])
+        hand_out(HALF + PIECE, accs[3])
         for q in range(4):
             queue = nc.sync if q % 2 == 0 else nc.scalar
             queue.dma_start(out=out_2[0, 4 * q : 4 * q + 4, :].bitcast(I32), in_=y_scales[32 * q : 32 * q + 4, :].bitcast(I32))

@@ -1,4 +1,3 @@
-import math
 from contextlib import ExitStack
 
 import concourse.mybir as mybir
@@ -22,7 +21,7 @@ LANES = 16
 HALF = S // 2
 PIECE = 128
 P_LOW, P_HIGH = 0.05, 0.95
-LOGIT_HIGH = math.log(P_HIGH / P_LOW)
+W2_ROW = 4
 
 
 def words_view(dram):
@@ -34,6 +33,12 @@ def load_scale_quadrant(queue, plane, dram, q):
     queue.dma_start(
         out=plane[32 * q : 32 * (q + 1), :].bitcast(I32),
         in_=rows.unsqueeze(0).to_broadcast([8, 4, rows.shape[1]]),
+    )
+
+
+def load_scale_rows(nc, plane, first, dram, q):
+    nc.sync.dma_start(
+        out=plane[32 * q + first : 32 * q + first + 4, :].bitcast(I32), in_=dram[0, 4 * q : 4 * q + 4, :].bitcast(I32)
     )
 
 
@@ -70,40 +75,40 @@ def tile_picked_focalpair_none_po_kernel(
         xw = keep.tile([P, T], I32, align_bytes=64)
         xs = keep.tile([P, T], U8, align_bytes=64)
         w1_raw = keep.tile([P, H], I32, align_bytes=64)
-        w1s_raw = keep.tile([P, H], U8, align_bytes=64)
         w2_raw = keep.tile([P, N], I32, align_bytes=64)
-        w2s_raw = keep.tile([P, N], U8, align_bytes=64)
+        ws_raw = keep.tile([P, H], U8, align_bytes=64)
         gain = keep.tile([P, PACK], F32)
         one = keep.tile([P, 1], F32)
+        nc.vector.memset(ws_raw[:].bitcast(I32), 0)
         nc.vector.memset(one[:], 1.0)
 
         nc.sync.dma_start(offs_sb[:], offs)
-        load_scale_quadrant(nc.sync, w1s_raw, w1_scales, 0)
         for q in range(4):
             load_scale_quadrant(nc.sync, xs, x_scales, q)
+        for q in range(2):
+            load_scale_rows(nc, ws_raw, 0, w1_scales, q)
         nc.sync.dma_start(out=xw[:], in_=words_view(x_words))
+        for q in range(2, 4):
+            load_scale_rows(nc, ws_raw, 0, w1_scales, q)
+        for q in range(4):
+            load_scale_rows(nc, ws_raw, W2_ROW, w2_scales, q)
         nc.sync.dma_start(out=w1_raw[:], in_=words_view(w1_words))
-        for q in range(1, 4):
-            load_scale_quadrant(nc.sync, w1s_raw, w1_scales, q)
         nc.sync.dma_start(pos_sb[:], pos)
         nc.sync.dma_start(out=w2_raw[:], in_=words_view(w2_words))
-        for q in range(4):
-            load_scale_quadrant(nc.sync, w2s_raw, w2_scales, q)
         nc.sync.dma_start(out=gain[:], in_=gn.rearrange("(p t) o -> p (t o)", t=PACK))
         nc.sync.dma_start(neg_sb[:], neg)
 
         w1 = keep.tile([P, H], I32, align_bytes=64)
-        w1s = keep.tile([P, H], U8, align_bytes=64)
         w2 = keep.tile([P, N], I32, align_bytes=64)
-        w2s = keep.tile([P, N], U8, align_bytes=64)
+        ws = keep.tile([P, H], U8, align_bytes=64)
         xg = keep.tile([P, S], U32, align_bytes=64)
         xgs = keep.tile([P, S], U8, align_bytes=64)
 
         nc.vector.tensor_copy(xgs[:], xs[:].indirect(offs_sb[:]))
-        deal_columns(nc, w1s, w1s_raw, 16)
         nc.vector.tensor_copy(xg[:], xw[:].bitcast(U32).indirect(offs_sb[:]))
-        deal_columns(nc, w1, w1_raw, 4, slice(0, 2))
-        deal_columns(nc, w1, w1_raw, 4, slice(2, 4))
+        for tiles in (slice(0, 1), slice(1, PACK)):
+            deal_columns(nc, ws, ws_raw, 16, tiles)
+            deal_columns(nc, w1, w1_raw, 4, tiles)
 
         h = [psum.tile([P, S], F32, name="h") for t in range(PACK)]
         for t in range(PACK):
@@ -111,57 +116,65 @@ def tile_picked_focalpair_none_po_kernel(
             nc.tensor.matmul_mx(
                 out=h[t][:],
                 lhsT=w1[:, feat].bitcast(FP8X4),
-                lhsT_scale=w1s[:, feat],
+                lhsT_scale=ws[:, feat],
                 rhs=xg[:].bitcast(FP8X4),
                 rhs_scale=xgs[:],
                 start=True,
                 stop=True,
             )
-
-        prob = [rows.tile([P, S], F32, name="prob") for t in range(PACK)]
-        p_pos = keep.tile([P, PACK, S], F32)
-        logit = keep.tile([P, S], F32)
-        nc.vector.tensor_scalar(logit[:], h[0][:], -LOGIT_HIGH, LOGIT_HIGH, ALU.max, ALU.min)
-        for t in range(1, PACK):
-            sig = rows.tile([P, S], F32)
-            nc.scalar.activation(sig[:], h[t][:], ACT.Sigmoid)
-            nc.vector.tensor_scalar(prob[t][:], sig[:], P_LOW, P_HIGH, ALU.max, ALU.min)
-            for lo in range(0, S, HALF):
-                nc.vector.tensor_copy(p_pos[:, t, lo : lo + HALF], prob[t][:].indirect(list_slice(pos_sb, lo, HALF)))
-        nc.scalar.activation(prob[0][:], logit[:], ACT.Sigmoid)
-        for lo in range(0, S, HALF):
-            nc.scalar.activation(p_pos[:, 0, lo : lo + HALF], logit[:].indirect(list_slice(pos_sb, lo, HALF)), ACT.Sigmoid)
-
         deal_columns(nc, w2, w2_raw, 4)
-        deal_columns(nc, w2s, w2s_raw, 16)
 
-        def positive_factors(log_p, w_sq, src):
-            nc.scalar.activation(log_p, src, ACT.Ln)
-            nc.scalar.activation(w_sq, src, ACT.Square, bias=one[:], scale=-1.0)
+        prob = [rows.tile([P, 2 * S], F32, name="prob") for t in range(PACK)]
+        picked = keep.tile([P, PACK + 1, S], F32)
 
-        def gained_product(out, square, log, t):
-            nc.vector.scalar_tensor_tensor(out, square, gain[:, t : t + 1], log, ALU.mult, ALU.mult)
+        def pick_positive(t):
+            nc.vector.tensor_copy(picked[:, t, :], prob[t][:].indirect(pos_sb[:]))
+
+        for t in range(PACK):
+            raw = prob[(t - 1) % PACK][:, S:]
+            nc.scalar.activation(raw, h[t][:], ACT.Sigmoid)
+            nc.vector.tensor_scalar(prob[t][:, :S], raw, P_LOW, P_HIGH, ALU.max, ALU.min)
+            if t > 0:
+                pick_positive(t - 1)
+        pick_positive(PACK - 1)
 
         log_p = keep.tile([P, PACK, S], F32)
         w_sq = keep.tile([P, PACK, S], F32)
         pos_term = keep.tile([P, PACK, S], F32)
-        z = keep.tile([P, PACK, S], F32)
         neg_term = [rows.tile([P, S], F32, name="neg_term") for t in range(PACK)]
 
+        def positive_log(tiles, cols):
+            nc.scalar.activation(log_p[:, tiles, cols], picked[:, tiles, cols], ACT.Ln)
+
+        def positive_square(tiles, cols):
+            nc.scalar.activation(w_sq[:, tiles, cols], picked[:, tiles, cols], ACT.Square, bias=one[:], scale=-1.0)
+
+        def gained_product(out, square, log, t):
+            nc.vector.scalar_tensor_tensor(out, square, gain[:, t : t + 1], log, ALU.mult, ALU.mult)
+
+        def positive_term(t, cols):
+            gained_product(pos_term[:, t, cols], w_sq[:, t, cols], log_p[:, t, cols], t)
+
         def difference(t, lo, count):
-            cols = slice(lo, lo + count)
+            at = lo % HALF
             nc.vector.tensor_tensor(
-                z[:, t, cols], neg_term[t][:].indirect(list_slice(neg_sb, lo, count)), pos_term[:, t, cols], ALU.subtract
+                picked[:, t + 1, at : at + count],
+                neg_term[t][:].indirect(list_slice(neg_sb, lo, count)),
+                pos_term[:, t, lo : lo + count],
+                ALU.subtract,
             )
 
         y_codes = keep.tile([P, S], I32, align_bytes=64)
         y_scales = keep.tile([P, S], U8, align_bytes=64)
         out_rows = out_0.rearrange("(p t) j -> p t j", t=PACK)
 
-        def second_layer(lo, cast):
-            cols = slice(lo, lo + PIECE)
+        def round_z(piece):
+            at = piece * PIECE % HALF
             z_bf = rows.tile([P, PIECE, PACK], BF16, align_bytes=64)
-            interleave(cast, z_bf[:], z[:, :, cols])
+            interleave(nc.scalar.copy, z_bf[:], picked[:, 1:, at : at + PIECE])
+            return z_bf
+
+        def second_layer(z_bf):
             z_codes = rows.tile([P, PIECE], I32, align_bytes=64)
             z_scales = rows.tile([P, PIECE], U8, align_bytes=64)
             nc.vector.quantize_mx(
@@ -173,7 +186,7 @@ def tile_picked_focalpair_none_po_kernel(
                 nc.tensor.matmul_mx(
                     out=acc[:, t, :],
                     lhsT=w2[:, feat].bitcast(FP8X4),
-                    lhsT_scale=w2s[:, feat],
+                    lhsT_scale=ws[W2_ROW:, feat],
                     rhs=z_codes[:].bitcast(FP8X4),
                     rhs_scale=z_scales[:],
                     start=True,
@@ -181,43 +194,55 @@ def tile_picked_focalpair_none_po_kernel(
                 )
             return acc
 
-        def hand_out(lo, acc):
-            cols = slice(lo, lo + PIECE)
+        def hand_out(piece, acc):
+            cols = slice(piece * PIECE, (piece + 1) * PIECE)
             y = rows.tile([P, PACK, PIECE], F32)
             nc.scalar.copy(out=y[:], in_=acc[:])
             nc.sync.dma_start(out=out_rows[:, :, cols], in_=y[:])
             y_bf = rows.tile([P, PIECE, PACK], BF16, align_bytes=64)
-            if lo < HALF:
-                nc.scalar.copy(out=y_bf[:], in_=acc[:].rearrange("p t j -> p j t"))
-            else:
-                interleave(nc.vector.tensor_copy, y_bf[:], y[:])
+            interleave(nc.vector.tensor_copy, y_bf[:], y[:])
             nc.vector.quantize_mx(
                 out=y_codes[:, cols].bitcast(FP8X4), scales=y_scales[:, cols], in_=y_bf[:].rearrange("p j t -> p (j t)")
             )
             nc.sync.dma_start(out=words_view(out_1)[:, cols], in_=y_codes[:, cols])
 
-        first, second = slice(0, HALF), slice(HALF, S)
-        for t in (1, 2, 3, 0):
-            log_q = rows.tile([P, S], F32)
-            nc.scalar.activation(log_q[:], prob[t][:], ACT.Ln, bias=one[:], scale=-1.0)
-            p_sq = rows.tile([P, S], F32)
-            nc.scalar.activation(p_sq[:], prob[t][:], ACT.Square)
-            gained_product(neg_term[t][:], p_sq[:], log_q[:], t)
-            positive_factors(log_p[:, t, first], w_sq[:, t, first], p_pos[:, t, first])
-            gained_product(pos_term[:, t, first], w_sq[:, t, first], log_p[:, t, first], t)
-            difference(t, 0, HALF)
-        accs = [second_layer(lo, nc.vector.tensor_copy) for lo in (0, PIECE)]
-        positive_factors(log_p[:, :, second], w_sq[:, :, second], p_pos[:, :, second])
+        first = slice(0, HALF)
+        third, fourth = slice(HALF, HALF + PIECE), slice(HALF + PIECE, S)
+        every = slice(0, PACK)
         for t in range(PACK):
-            gained_product(pos_term[:, t, second], w_sq[:, t, second], log_p[:, t, second], t)
+            log_q = rows.tile([P, S], F32)
+            nc.scalar.activation(log_q[:], prob[t][:, :S], ACT.Ln, bias=one[:], scale=-1.0)
+            p_sq = rows.tile([P, S], F32)
+            nc.scalar.activation(p_sq[:], prob[t][:, :S], ACT.Square)
+            gained_product(neg_term[t][:], p_sq[:], log_q[:], t)
+            positive_log(t, first)
+            positive_square(t, first)
+            positive_term(t, first)
+            if t > 0:
+                difference(t - 1, 0, HALF)
+        difference(PACK - 1, 0, HALF)
+
+        positive_log(every, third)
+        positive_square(every, third)
+        for t in range(PACK):
+            positive_term(t, third)
+        positive_log(every, fourth)
+        accs = [second_layer(round_z(0))]
+        for t in range(PACK):
+            difference(t, HALF, PIECE)
+        positive_square(every, fourth)
+        z_bf = round_z(1)
+        for t in range(PACK):
+            positive_term(t, fourth)
+        accs.append(second_layer(z_bf))
+        for t in range(PACK):
+            difference(t, HALF + PIECE, PIECE)
+        accs.append(second_layer(round_z(2)))
         hand_out(0, accs[0])
-        hand_out(PIECE, accs[1])
-        for lo, cast in ((HALF, nc.scalar.copy), (HALF + PIECE, nc.vector.tensor_copy)):
-            for t in range(PACK):
-                difference(t, lo, PIECE)
-            accs.append(second_layer(lo, cast))
-        hand_out(HALF, accs[2])
-        hand_out(HALF + PIECE, accs[3])
+        hand_out(1, accs[1])
+        accs.append(second_layer(round_z(3)))
+        hand_out(2, accs[2])
+        hand_out(3, accs[3])
         for q in range(4):
             queue = nc.sync if q % 2 == 0 else nc.scalar
             queue.dma_start(out=out_2[0, 4 * q : 4 * q + 4, :].bitcast(I32), in_=y_scales[32 * q : 32 * q + 4, :].bitcast(I32))

@@ -28,16 +28,8 @@ def words_view(dram):
     return dram[0].rearrange("p c r -> p (c r)").bitcast(I32)
 
 
-def load_scale_quadrant(queue, plane, dram, q):
-    rows = dram[0, 4 * q : 4 * q + 4, :].bitcast(I32)
+def load_scale_rows(queue, plane, first, dram, q):
     queue.dma_start(
-        out=plane[32 * q : 32 * (q + 1), :].bitcast(I32),
-        in_=rows.unsqueeze(0).to_broadcast([8, 4, rows.shape[1]]),
-    )
-
-
-def load_scale_rows(nc, plane, first, dram, q):
-    nc.sync.dma_start(
         out=plane[32 * q + first : 32 * q + first + 4, :].bitcast(I32), in_=dram[0, 4 * q : 4 * q + 4, :].bitcast(I32)
     )
 
@@ -79,20 +71,19 @@ def tile_picked_focalpair_none_po_kernel(
         ws_raw = keep.tile([P, H], U8, align_bytes=64)
         gain = keep.tile([P, PACK], F32)
         one = keep.tile([P, 1], F32)
+        nc.vector.memset(xs[:].bitcast(I32), 0)
         nc.vector.memset(ws_raw[:].bitcast(I32), 0)
         nc.vector.memset(one[:], 1.0)
 
         nc.sync.dma_start(offs_sb[:], offs)
-        for q in range(4):
-            load_scale_quadrant(nc.sync, xs, x_scales, q)
-        for q in range(2):
-            load_scale_rows(nc, ws_raw, 0, w1_scales, q)
-        nc.sync.dma_start(out=xw[:], in_=words_view(x_words))
-        for q in range(2, 4):
-            load_scale_rows(nc, ws_raw, 0, w1_scales, q)
-        for q in range(4):
-            load_scale_rows(nc, ws_raw, W2_ROW, w2_scales, q)
         nc.sync.dma_start(out=w1_raw[:], in_=words_view(w1_words))
+        for q in range(4):
+            load_scale_rows(nc.sync, xs, 0, x_scales, q)
+        nc.sync.dma_start(out=xw[:], in_=words_view(x_words))
+        for q in range(4):
+            load_scale_rows(nc.sync, ws_raw, 0, w1_scales, q)
+        for q in range(4):
+            load_scale_rows(nc.sync if q < 3 else nc.gpsimd, ws_raw, W2_ROW, w2_scales, q)
         nc.sync.dma_start(pos_sb[:], pos)
         nc.sync.dma_start(out=w2_raw[:], in_=words_view(w2_words))
         nc.sync.dma_start(out=gain[:], in_=gn.rearrange("(p t) o -> p (t o)", t=PACK))
@@ -105,10 +96,10 @@ def tile_picked_focalpair_none_po_kernel(
         xgs = keep.tile([P, S], U8, align_bytes=64)
 
         nc.vector.tensor_copy(xgs[:], xs[:].indirect(offs_sb[:]))
+        deal_columns(nc, w1, w1_raw, 4)
         nc.vector.tensor_copy(xg[:], xw[:].bitcast(U32).indirect(offs_sb[:]))
         for tiles in (slice(0, 1), slice(1, PACK)):
             deal_columns(nc, ws, ws_raw, 16, tiles)
-            deal_columns(nc, w1, w1_raw, 4, tiles)
 
         h = [psum.tile([P, S], F32, name="h") for t in range(PACK)]
         for t in range(PACK):

@@ -59,7 +59,7 @@ def tile_picked_focalpair_none_po_kernel(
     with ExitStack() as ctx:
         keep = ctx.enter_context(tc.tile_pool(name="keep", bufs=1))
         rows = ctx.enter_context(tc.tile_pool(name="rows", bufs=PACK))
-        psum = ctx.enter_context(tc.psum_pool(name="psum", bufs=PACK))
+        psum = ctx.enter_context(tc.psum_pool(name="psum", bufs=2 * PACK))
 
         offs_sb = keep.tile([P, S // LANES], U16)
         pos_sb = keep.tile([P, S // LANES], U16)
@@ -79,11 +79,12 @@ def tile_picked_focalpair_none_po_kernel(
         nc.sync.dma_start(out=w1_raw[:], in_=words_view(w1_words))
         for q in range(4):
             load_scale_rows(nc.sync, xs, 0, x_scales, q)
+        load_scale_rows(nc.sync, ws_raw, 0, w1_scales, 0)
         nc.sync.dma_start(out=xw[:], in_=words_view(x_words))
-        for q in range(4):
+        for q in range(1, 4):
             load_scale_rows(nc.sync, ws_raw, 0, w1_scales, q)
         for q in range(4):
-            load_scale_rows(nc.sync if q < 3 else nc.gpsimd, ws_raw, W2_ROW, w2_scales, q)
+            load_scale_rows(nc.sync, ws_raw, W2_ROW, w2_scales, q)
         nc.sync.dma_start(pos_sb[:], pos)
         nc.sync.dma_start(out=w2_raw[:], in_=words_view(w2_words))
         nc.sync.dma_start(out=gain[:], in_=gn.rearrange("(p t) o -> p (t o)", t=PACK))
@@ -155,27 +156,30 @@ def tile_picked_focalpair_none_po_kernel(
                 ALU.subtract,
             )
 
+        out_rows = out_0.rearrange("(p t) j -> p t j", t=PACK)
+        y = keep.tile([P, PACK, S], F32)
         y_codes = keep.tile([P, S], I32, align_bytes=64)
         y_scales = keep.tile([P, S], U8, align_bytes=64)
-        out_rows = out_0.rearrange("(p t) j -> p t j", t=PACK)
 
-        def round_z(piece):
+        def round_z(piece, copies):
             at = piece * PIECE % HALF
-            z_bf = rows.tile([P, PIECE, PACK], BF16, align_bytes=64)
-            interleave(nc.scalar.copy, z_bf[:], picked[:, 1:, at : at + PIECE])
-            return z_bf
+            share = PIECE // len(copies)
+            for part, copy in enumerate(copies):
+                lo = part * share
+                interleave(copy, z_bf[piece][:, lo : lo + share, :], picked[:, 1:, at + lo : at + lo + share])
 
-        def second_layer(z_bf):
+        def second_layer(z_bf, banks):
             z_codes = rows.tile([P, PIECE], I32, align_bytes=64)
             z_scales = rows.tile([P, PIECE], U8, align_bytes=64)
             nc.vector.quantize_mx(
                 out=z_codes[:].bitcast(FP8X4), scales=z_scales[:], in_=z_bf[:].rearrange("p j t -> p (j t)")
             )
-            acc = psum.tile([P, PACK, PIECE], F32)
+            share = PACK // banks
+            accs = [psum.tile([P, share, PIECE], F32, name="h") for bank in range(banks)]
             for t in range(PACK):
                 feat = slice(t * P, (t + 1) * P)
                 nc.tensor.matmul_mx(
-                    out=acc[:, t, :],
+                    out=accs[t // share][:, t % share, :],
                     lhsT=w2[:, feat].bitcast(FP8X4),
                     lhsT_scale=ws[W2_ROW:, feat],
                     rhs=z_codes[:].bitcast(FP8X4),
@@ -183,20 +187,28 @@ def tile_picked_focalpair_none_po_kernel(
                     start=True,
                     stop=True,
                 )
-            return acc
+            return accs
 
-        def hand_out(piece, acc):
+        def hand_out(piece, queue):
             cols = slice(piece * PIECE, (piece + 1) * PIECE)
-            y = rows.tile([P, PACK, PIECE], F32)
-            nc.scalar.copy(out=y[:], in_=acc[:])
-            nc.sync.dma_start(out=out_rows[:, :, cols], in_=y[:])
-            y_bf = rows.tile([P, PIECE, PACK], BF16, align_bytes=64)
-            interleave(nc.vector.tensor_copy, y_bf[:], y[:])
+            share = PACK // len(accs[piece])
+            for bank, acc in enumerate(accs[piece]):
+                nc.scalar.copy(out=y[:, bank * share : (bank + 1) * share, cols], in_=acc[:])
+            queue.dma_start(out=out_rows[:, :, cols], in_=y[:, :, cols])
+
+        def round_y(y_bf, piece):
+            interleave(nc.vector.tensor_copy, y_bf, y[:, :, piece * PIECE : (piece + 1) * PIECE])
+
+        def quantize_y(y_bf, cols):
             nc.vector.quantize_mx(
                 out=y_codes[:, cols].bitcast(FP8X4), scales=y_scales[:, cols], in_=y_bf[:].rearrange("p j t -> p (j t)")
             )
+
+        def store_codes(cols):
             nc.sync.dma_start(out=words_view(out_1)[:, cols], in_=y_codes[:, cols])
 
+        z_bf = [rows.tile([P, PIECE, PACK], BF16, align_bytes=64, name="z_bf") for piece in range(3)]
+        z_bf.append(keep.tile([P, PIECE, PACK], BF16, align_bytes=64, name="last"))
         first = slice(0, HALF)
         third, fourth = slice(HALF, HALF + PIECE), slice(HALF + PIECE, S)
         every = slice(0, PACK)
@@ -218,22 +230,37 @@ def tile_picked_focalpair_none_po_kernel(
         for t in range(PACK):
             positive_term(t, third)
         positive_log(every, fourth)
-        accs = [second_layer(round_z(0))]
+        round_z(0, [nc.scalar.copy])
+        accs = [second_layer(z_bf[0], 1)]
         for t in range(PACK):
             difference(t, HALF, PIECE)
         positive_square(every, fourth)
-        z_bf = round_z(1)
+        round_z(1, [nc.scalar.copy])
         for t in range(PACK):
             positive_term(t, fourth)
-        accs.append(second_layer(z_bf))
+        accs.append(second_layer(z_bf[1], 1))
         for t in range(PACK):
             difference(t, HALF + PIECE, PIECE)
-        accs.append(second_layer(round_z(2)))
-        hand_out(0, accs[0])
-        hand_out(1, accs[1])
-        accs.append(second_layer(round_z(3)))
-        hand_out(2, accs[2])
-        hand_out(3, accs[3])
+        round_z(2, [nc.scalar.copy])
+        accs.append(second_layer(z_bf[2], 1))
+        hand_out(0, nc.sync)
+        hand_out(1, nc.sync)
+        y_first = keep.tile([P, PIECE, PACK], BF16, align_bytes=64)
+        nc.scalar.copy(out=y_first[:], in_=accs[0][0][:].rearrange("p t j -> p j t"))
+        round_z(3, [nc.scalar.copy, nc.vector.tensor_copy])
+        quantize_y(y_first, slice(0, PIECE))
+        accs.append(second_layer(z_bf[3], 2))
+        y_middle = keep.tile([P, 2 * PIECE, PACK], BF16, align_bytes=64, name="last")
+        round_y(y_middle[:, :PIECE, :], 1)
+        hand_out(2, nc.sync)
+        round_y(y_middle[:, PIECE:, :], 2)
+        quantize_y(y_middle, slice(PIECE, 3 * PIECE))
+        store_codes(slice(0, 3 * PIECE))
+        hand_out(3, nc.scalar)
+        y_last = keep.tile([P, PIECE, PACK], BF16, align_bytes=64)
+        round_y(y_last[:], 3)
+        quantize_y(y_last, fourth)
+        store_codes(fourth)
         for q in range(4):
             queue = nc.sync if q % 2 == 0 else nc.scalar
             queue.dma_start(out=out_2[0, 4 * q : 4 * q + 4, :].bitcast(I32), in_=y_scales[32 * q : 32 * q + 4, :].bitcast(I32))

from contextlib import ExitStack

import concourse.mybir as mybir

K, T, S, N, H = 512, 2048, 512, 512, 512
FLOPS = 2 * K * H * S + 2 * H * N * S

F32 = mybir.dt.float32
BF16 = mybir.dt.bfloat16
I32 = mybir.dt.int32
U32 = mybir.dt.uint32
U16 = mybir.dt.uint16
U8 = mybir.dt.uint8
FP8X4 = mybir.dt.float8_e4m3fn_x4
ALU = mybir.AluOpType
ACT = mybir.ActivationFunctionType

P = 128
PACK = 4
LANES = 16
HALF = S // 2
PIECE = 128
P_LOW, P_HIGH = 0.05, 0.95
W2_ROW = 4


def words_view(dram):
    return dram[0].rearrange("p c r -> p (c r)").bitcast(I32)


def load_scale_rows(queue, plane, first, dram, q):
    queue.dma_start(
        out=plane[32 * q + first : 32 * q + first + 4, :].bitcast(I32), in_=dram[0, 4 * q : 4 * q + 4, :].bitcast(I32)
    )


def deal_columns(nc, dst, src, run, tiles=slice(0, PACK)):
    nc.vector.tensor_copy(
        out=dst[:].rearrange("p (t c i) -> p c t i", t=PACK, i=run)[:, :, tiles, :],
        in_=src[:].rearrange("p (c i t) -> p c t i", t=PACK, i=run)[:, :, tiles, :],
    )


def interleave(engine_copy, dst, src):
    engine_copy(
        out=dst.rearrange("p (c i) t -> p c t i", i=4),
        in_=src.rearrange("p t (c i) -> p c t i", i=4),
    )


def list_slice(lst, start, count):
    return lst[:, start // LANES : (start + count) // LANES]


def tile_picked_focalpair_none_po_kernel(
    tc, x_words, x_scales, w1_words, w1_scales, gn, w2_words, w2_scales, offs, pos, neg, out_0, out_1, out_2
):
    nc = tc.nc
    with ExitStack() as ctx:
        keep = ctx.enter_context(tc.tile_pool(name="keep", bufs=1))
        rows = ctx.enter_context(tc.tile_pool(name="rows", bufs=PACK))
        psum = ctx.enter_context(tc.psum_pool(name="psum", bufs=2 * PACK))

        offs_sb = keep.tile([P, S // LANES], U16)
        pos_sb = keep.tile([P, S // LANES], U16)
        neg_sb = keep.tile([P, S // LANES], U16)
        xw = keep.tile([P, T], I32, align_bytes=64)
        xs = keep.tile([P, T], U8, align_bytes=64)
        w1_raw = keep.tile([P, H], I32, align_bytes=64)
        w2_raw = keep.tile([P, N], I32, align_bytes=64)
        ws_raw = keep.tile([P, H], U8, align_bytes=64)
        gain = keep.tile([P, PACK], F32)
        one = keep.tile([P, 1], F32)
        nc.vector.memset(xs[:].bitcast(I32), 0)
        nc.vector.memset(ws_raw[:].bitcast(I32), 0)
        nc.vector.memset(one[:], 1.0)

        nc.sync.dma_start(offs_sb[:], offs)
        nc.sync.dma_start(out=w1_raw[:], in_=words_view(w1_words))
        for q in range(4):
            load_scale_rows(nc.sync, xs, 0, x_scales, q)
        load_scale_rows(nc.sync, ws_raw, 0, w1_scales, 0)
        nc.sync.dma_start(out=xw[:], in_=words_view(x_words))
        for q in range(1, 4):
            load_scale_rows(nc.sync, ws_raw, 0, w1_scales, q)
        for q in range(4):
            load_scale_rows(nc.sync, ws_raw, W2_ROW, w2_scales, q)
        nc.sync.dma_start(pos_sb[:], pos)
        nc.sync.dma_start(out=w2_raw[:], in_=words_view(w2_words))
        nc.sync.dma_start(out=gain[:], in_=gn.rearrange("(p t) o -> p (t o)", t=PACK))
        nc.sync.dma_start(neg_sb[:], neg)

        w1 = keep.tile([P, H], I32, align_bytes=64)
        w2 = keep.tile([P, N], I32, align_bytes=64)
        ws = keep.tile([P, H], U8, align_bytes=64)
        xg = keep.tile([P, S], U32, align_bytes=64)
        xgs = keep.tile([P, S], U8, align_bytes=64)

        nc.vector.tensor_copy(xgs[:], xs[:].indirect(offs_sb[:]))
        deal_columns(nc, w1, w1_raw, 4)
        nc.vector.tensor_copy(xg[:], xw[:].bitcast(U32).indirect(offs_sb[:]))
        for tiles in (slice(0, 1), slice(1, PACK)):
            deal_columns(nc, ws, ws_raw, 16, tiles)

        h = [psum.tile([P, S], F32, name="h") for t in range(PACK)]
        for t in range(PACK):
            feat = slice(t * P, (t + 1) * P)
            nc.tensor.matmul_mx(
                out=h[t][:],
                lhsT=w1[:, feat].bitcast(FP8X4),
                lhsT_scale=ws[:, feat],
                rhs=xg[:].bitcast(FP8X4),
                rhs_scale=xgs[:],
                start=True,
                stop=True,
            )
        deal_columns(nc, w2, w2_raw, 4)

        prob = [rows.tile([P, 2 * S], F32, name="prob") for t in range(PACK)]
        picked = keep.tile([P, PACK + 1, S], F32)

        def pick_positive(t):
            nc.vector.tensor_copy(picked[:, t, :], prob[t][:].indirect(pos_sb[:]))

        for t in range(PACK):
            raw = prob[(t - 1) % PACK][:, S:]
            nc.scalar.activation(raw, h[t][:], ACT.Sigmoid)
            nc.vector.tensor_scalar(prob[t][:, :S], raw, P_LOW, P_HIGH, ALU.max, ALU.min)
            if t > 0:
                pick_positive(t - 1)
        pick_positive(PACK - 1)

        log_p = keep.tile([P, PACK, S], F32)
        w_sq = keep.tile([P, PACK, S], F32)
        pos_term = keep.tile([P, PACK, S], F32)
        neg_term = [rows.tile([P, S], F32, name="neg_term") for t in range(PACK)]

        def positive_log(tiles, cols):
            nc.scalar.activation(log_p[:, tiles, cols], picked[:, tiles, cols], ACT.Ln)

        def positive_square(tiles, cols):
            nc.scalar.activation(w_sq[:, tiles, cols], picked[:, tiles, cols], ACT.Square, bias=one[:], scale=-1.0)

        def gained_product(out, square, log, t):
            nc.vector.scalar_tensor_tensor(out, square, gain[:, t : t + 1], log, ALU.mult, ALU.mult)

        def positive_term(t, cols):
            gained_product(pos_term[:, t, cols], w_sq[:, t, cols], log_p[:, t, cols], t)

        def difference(t, lo, count):
            at = lo % HALF
            nc.vector.tensor_tensor(
                picked[:, t + 1, at : at + count],
                neg_term[t][:].indirect(list_slice(neg_sb, lo, count)),
                pos_term[:, t, lo : lo + count],
                ALU.subtract,
            )

        out_rows = out_0.rearrange("(p t) j -> p t j", t=PACK)
        y = keep.tile([P, PACK, S], F32)
        y_codes = keep.tile([P, S], I32, align_bytes=64)
        y_scales = keep.tile([P, S], U8, align_bytes=64)

        def round_z(piece, copies):
            at = piece * PIECE % HALF
            share = PIECE // len(copies)
            for part, copy in enumerate(copies):
                lo = part * share
                interleave(copy, z_bf[piece][:, lo : lo + share, :], picked[:, 1:, at + lo : at + lo + share])

        def second_layer(z_bf, banks):
            z_codes = rows.tile([P, PIECE], I32, align_bytes=64)
            z_scales = rows.tile([P, PIECE], U8, align_bytes=64)
            nc.vector.quantize_mx(
                out=z_codes[:].bitcast(FP8X4), scales=z_scales[:], in_=z_bf[:].rearrange("p j t -> p (j t)")
            )
            share = PACK // banks
            accs = [psum.tile([P, share, PIECE], F32, name="h") for bank in range(banks)]
            for t in range(PACK):
                feat = slice(t * P, (t + 1) * P)
                nc.tensor.matmul_mx(
                    out=accs[t // share][:, t % share, :],
                    lhsT=w2[:, feat].bitcast(FP8X4),
                    lhsT_scale=ws[W2_ROW:, feat],
                    rhs=z_codes[:].bitcast(FP8X4),
                    rhs_scale=z_scales[:],
                    start=True,
                    stop=True,
                )
            return accs

        def hand_out(piece, queue):
            cols = slice(piece * PIECE, (piece + 1) * PIECE)
            share = PACK // len(accs[piece])
            for bank, acc in enumerate(accs[piece]):
                nc.scalar.copy(out=y[:, bank * share : (bank + 1) * share, cols], in_=acc[:])
            queue.dma_start(out=out_rows[:, :, cols], in_=y[:, :, cols])

        def round_y(y_bf, piece):
            interleave(nc.vector.tensor_copy, y_bf, y[:, :, piece * PIECE : (piece + 1) * PIECE])

        def quantize_y(y_bf, cols):
            nc.vector.quantize_mx(
                out=y_codes[:, cols].bitcast(FP8X4), scales=y_scales[:, cols], in_=y_bf[:].rearrange("p j t -> p (j t)")
            )

        def store_codes(cols):
            nc.sync.dma_start(out=words_view(out_1)[:, cols], in_=y_codes[:, cols])

        z_bf = [rows.tile([P, PIECE, PACK], BF16, align_bytes=64, name="z_bf") for piece in range(3)]
        z_bf.append(keep.tile([P, PIECE, PACK], BF16, align_bytes=64, name="last"))
        first = slice(0, HALF)
        third, fourth = slice(HALF, HALF + PIECE), slice(HALF + PIECE, S)
        every = slice(0, PACK)
        for t in range(PACK):
            log_q = rows.tile([P, S], F32)
            nc.scalar.activation(log_q[:], prob[t][:, :S], ACT.Ln, bias=one[:], scale=-1.0)
            p_sq = rows.tile([P, S], F32)
            nc.scalar.activation(p_sq[:], prob[t][:, :S], ACT.Square)
            gained_product(neg_term[t][:], p_sq[:], log_q[:], t)
            positive_log(t, first)
            positive_square(t, first)
            positive_term(t, first)
            if t > 0:
                difference(t - 1, 0, HALF)
        difference(PACK - 1, 0, HALF)

        positive_log(every, third)
        positive_square(every, third)
        for t in range(PACK):
            positive_term(t, third)
        positive_log(every, fourth)
        round_z(0, [nc.scalar.copy])
        accs = [second_layer(z_bf[0], 1)]
        for t in range(PACK):
            difference(t, HALF, PIECE)
        positive_square(every, fourth)
        round_z(1, [nc.scalar.copy])
        for t in range(PACK):
            positive_term(t, fourth)
        accs.append(second_layer(z_bf[1], 1))
        for t in range(PACK):
            difference(t, HALF + PIECE, PIECE)
        round_z(2, [nc.scalar.copy])
        accs.append(second_layer(z_bf[2], 1))
        hand_out(0, nc.sync)
        hand_out(1, nc.sync)
        y_first = keep.tile([P, PIECE, PACK], BF16, align_bytes=64)
        nc.scalar.copy(out=y_first[:], in_=accs[0][0][:].rearrange("p t j -> p j t"))
        round_z(3, [nc.scalar.copy, nc.vector.tensor_copy])
        quantize_y(y_first, slice(0, PIECE))
        accs.append(second_layer(z_bf[3], 2))
        y_middle = keep.tile([P, 2 * PIECE, PACK], BF16, align_bytes=64, name="last")
        round_y(y_middle[:, :PIECE, :], 1)
        hand_out(2, nc.sync)
        round_y(y_middle[:, PIECE:, :], 2)
        quantize_y(y_middle, slice(PIECE, 3 * PIECE))
        store_codes(slice(0, 3 * PIECE))
        hand_out(3, nc.scalar)
        y_last = keep.tile([P, PIECE, PACK], BF16, align_bytes=64)
        round_y(y_last[:], 3)
        quantize_y(y_last, fourth)
        store_codes(fourth)
        for q in range(4):
            queue = nc.sync if q % 2 == 0 else nc.scalar
            queue.dma_start(out=out_2[0, 4 * q : 4 * q + 4, :].bitcast(I32), in_=y_scales[32 * q : 32 * q + 4, :].bitcast(I32))
